import numpy as np
CORES = [29,45,93,109,157,173,221,237,285,301,349,365,413,429,477,493]
N = 16
R, W, T = 8192, 64, 1024
CAPP = 128
def entries(a): return a.T.reshape(-1)
def pack(v, P): return np.ascontiguousarray(np.asarray(v, np.int32).reshape(-1, P).T)
def lists(rng, how):
    I = rng.integers(0, N * R, (N, T))
    O = np.stack([rng.permutation(np.repeat(np.arange(N), CAPP))[:T] for r in range(N)])
    if how == "full": O = np.stack([rng.permutation(np.repeat(rng.permutation(N)[:T // CAPP], CAPP)) for r in range(N)])
    I = R * O + rng.integers(0, R, (N, T))
    if how == "alike": I = R * O + rng.integers(0, R, (N, 1))
    if how == "edge": I = R * O + np.where(rng.random((N, T)) < 0.5, 0, R - 1)
    if how == "sorted": I = np.sort(I, axis=1)
    return {"idx": np.stack([pack(I[r], 128) for r in range(N)])}
def setup_inputs(rng):
    return dict({"tab": rng.standard_normal((N, R, W), dtype=np.float32)}, **lists(rng, "uniform"))
def setup_inputs_alike(rng):
    d = setup_inputs(rng); d.update(lists(rng, "alike"))
    for k in ("tab",): d[k] = (d[k].astype(np.float32) * 1048576.0).astype(d[k].dtype)
    return d
def setup_inputs_edge(rng):
    d = setup_inputs(rng); d.update(lists(rng, "edge"))
    for k in ("tab",): d[k] = (d[k].astype(np.float32) * (1 / 1024.0)).astype(d[k].dtype)
    return d
def setup_inputs_full(rng):
    d = setup_inputs(rng); d.update(lists(rng, "full"))
    return d
def setup_inputs_sorted(rng):
    d = setup_inputs(rng); d.update(lists(rng, "sorted"))
    return d
def check_inputs(x):
    bad = []
    if x["idx"].min() < 0 or x["idx"].max() >= N * R: bad.append("idx out of range")
    if max(int(np.bincount(entries(a) // R, minlength=N).max()) for a in x["idx"]) > CAPP: bad.append("more than CAPP entries of a list point into one rank's part")
    return bad
def reference(tab, idx):
    A = np.concatenate(list(tab), axis=0)
    return {"y": np.stack([A[entries(idx[r])] for r in range(N)])}

@@ -1,0 +1,401 @@
+from concourse.bass import DstId, RemoteDMATransfer
+from concourse.mybir import AluOpType, ActivationFunctionType
+
+NSIM = 512
+NF = 2
+NPOOL = 120
+GROUPS = [4, 4, 4, 4, 4, 4, 3, 2, 1, 1, 1]
+GBANK = [0, 1, 2, 3, 4, 5, 6, 7, 0, 1, 2]
+ON_SCALAR = [0, 1, 2, 4, 6, 8, 10]
+
+SCRATCH = {
+    "idx_s": ("sbuf", [128, 8], "int32"),
+    "raw": ("sbuf", [128, 4096], "float32"),
+    "win": ("sbuf", [128, 8192], "float32"),
+    "ident": ("sbuf", [128, 128], "float32"),
+    "d128": ("sbuf", [128, 128], "int32"),
+    "amod": ("sbuf", [128, 128], "int32"),
+    "a2": ("sbuf", [128, 256], "float32"),
+    "lstr": ("sbuf", [128, 128], "bfloat16"),
+    "ones": ("sbuf", [128, 128], "bfloat16"),
+    "io16": ("sbuf", [128, 16], "float32"),
+    "kpat": ("sbuf", [128, 128], "bfloat16"),
+    "rmask": ("sbuf", [128, 128], "bfloat16"),
+    "pat1": ("sbuf", [128, 128], "bfloat16"),
+    "patb": ("sbuf", [128, 64], "bfloat16"),
+    "v8": ("sbuf", [128, 8], "int32"),
+    "v8s": ("sbuf", [128, 8], "int32"),
+    "mask8": ("sbuf", [128, 8], "float32"),
+    "iw": ("sbuf", [128, 96], "int32"),
+    "fw": ("sbuf", [128, 104], "float32"),
+    "e2": ("sbuf", [128, 128], "bfloat16"),
+    "incl": ("sbuf", [128, 128], "bfloat16"),
+    "excl": ("sbuf", [128, 128], "bfloat16"),
+    "prod": ("sbuf", [128, 128], "float32"),
+    "tree": ("sbuf", [128, 112], "float32"),
+    "amat": ("sbuf", [128, 1024], "bfloat16"),
+    "bhi": ("sbuf", [128, 512], "bfloat16"),
+    "blo": ("sbuf", [128, 512], "bfloat16"),
+    "req16": ("sbuf", [128, 64], "uint16"),
+    "offs": ("sbuf", [128, 60], "uint16"),
+    "outb": ("sbuf", [128, 960], "float32"),
+    "land": ("sbuf", [128, 2048], "float32"),
+    "rhsf": ("sbuf", [128, 64], "float32"),
+    "foffs": ("sbuf", [128, 32], "uint16"),
+    "gat": ("sbuf", [128, 512], "float32"),
+    "ysb": ("sbuf", [128, 512], "float32"),
+    "rqf": ("sbuf", [128, 32 // NF], "uint16"),
+    "rsf": ("sbuf", [128, 512 // NF], "float32"),
+    "ps": ("psum", [128, 4096], "float32"),
+}
+SEMAPHORES = ["rqF", "rqN", "rsF", "rsN", "fq", "fr", "snt"] + ["s%d" % i for i in range(NPOOL)]
+
+_CACHE = {}
+
+
+def _plan(T, topo):
+    if "p" in _CACHE:
+        return _CACHE["p"]
+    cores = list(T.cores)
+    n = len(cores)
+    rk = [topo.rack(topo.host(c)) for c in cores]
+    far = [[d for d in range(n) if rk[d] != rk[r]] for r in range(n)]
+    near = [[d for d in range(n) if rk[d] == rk[r]] for r in range(n)]
+    peer = [[d for d in far[r] if topo.may_write(cores[r], cores[d]) and topo.chip(cores[d]) == topo.chip(cores[r])][0]
+            for r in range(n)]
+    helpers = []
+    fwd = {}
+    for r in range(n):
+        c0 = cores[r]
+        hs = [c for c in range(NSIM) if topo.host(c) == topo.host(c0) and topo.chip(c) == topo.chip(c0)
+              and c != c0 and topo.die(c) != topo.die(c0)][:NF]
+        helpers.append(hs)
+        for f, c in enumerate(hs):
+            fwd[c] = (r, f)
+    p = {"cores": cores, "far": far, "near": near, "peer": peer, "helpers": helpers, "fwd": fwd}
+    _CACHE["p"] = p
+    return p
+
+
+def _fused(g, core, topo, items, per, lsem):
+    m = 0xFFFF
+    for it in items:
+        m &= topo.mask(core, it[0])
+    e = [1 << b for b in range(16) if (m >> b) & 1]
+    trs = []
+    for i, (d, s, o, rs) in enumerate(items):
+        mk = 0
+        for b in e[i * per:(i + 1) * per]:
+            mk |= b
+        rid, pid = topo.addr(d, core)
+        trs.append(RemoteDMATransfer(dst_ids=[DstId(rid=rid, pnc=pid)], dma_engine_mask=mk, remote_sem=rs, src=s, dst=o))
+    g.remote_dma_fused(trs, local_sem=lsem)
+    return per * len(items)
+
+
+def _forwarder(g, core, T, topo, P, x, f):
+    s = P["peer"][x]
+    cores = P["cores"]
+    nb = 8 // NF
+    dsts = P["far"][s][f * nb:(f + 1) * nb]
+    per = 8 // nb
+    sent = 0
+    g.wait_ge(T.sem.fq, 8 // NF)
+    sent += _fused(g, core, topo, [(cores[o], T.rqf[:, i * 4:(i + 1) * 4],
+                                    T.offs[:, P["far"][o].index(s) * 4:P["far"][o].index(s) * 4 + 4], T.sem.rqF)
+                                   for i, o in enumerate(dsts)], per, T.sem.snt)
+    g.wait_ge(T.sem.fr, 8 // NF)
+    sent += _fused(g, core, topo, [(cores[q], T.rsf[:, i * 64:(i + 1) * 64], T.land[:, s * 64:(s + 1) * 64], T.sem.rsF)
+                                   for i, q in enumerate(dsts)], per, T.sem.snt)
+    g.wait_ge(T.sem.snt, sent)
+
+
+def rank_program(g, core, T, topo):
+    P = _plan(T, topo)
+    me = T.rank_of(core)
+    if me is None:
+        if core in P["fwd"]:
+            _forwarder(g, core, T, topo, P, P["fwd"][core][0], P["fwd"][core][1])
+        return
+    A = AluOpType
+    V, S, PE, SY = g.vector, g.scalar, g.tensor, g.sync
+    cores, far, near = P["cores"], P["far"][me], P["near"][me]
+    stages = []
+
+    def stage():
+        s = [T.sem["s%d" % len(stages)], 0]
+        stages.append(s)
+        return s
+
+    def done(ins, s, n=1):
+        ins.then_inc(s[0], n)
+        s[1] += n
+
+    def need(q, *ss):
+        for s in ss:
+            q.wait_ge(s[0], s[1])
+
+    def one(ins, n=1):
+        s = stage()
+        done(ins, s, n)
+        return s
+
+    def ts(out, in0, s1, op0, s2=None, op1=None):
+        if op1 is None:
+            return V.tensor_scalar(out, in0, s1, None, op0)
+        return V.tensor_scalar(out, in0, s1, s2, op0, op1)
+
+    def iw(i):
+        return T.iw[:, i * 8:(i + 1) * 8]
+
+    def fw(i):
+        return T.fw[:, i * 8:(i + 1) * 8]
+
+    def bank(b, n):
+        return T.ps[:, b * 512:b * 512 + n]
+
+    s_idx = one(SY.dma_start(T.idx_s[:], T.idx[:]), 16)
+    s_ld = []
+    for b in range(8):
+        q = SY if b % 2 == 0 else S
+        s_ld.append(one(q.dma_start(T.raw[:, b * 512:(b + 1) * 512], T.tab[b * 1024:(b + 1) * 1024, :]), 16))
+
+    s_d = one(g.iota(T.d128[:], [[1, 128]], 128, -1))
+    s_io = one(g.iota(T.io16[:], [[1, 16]], 0, 0, allow_small_or_imprecise_dtypes=True))
+    s_kp = one(g.iota(T.kpat[:], [[0, 16], [1, 8]], 0, 0, allow_small_or_imprecise_dtypes=True))
+    s_p1 = one(g.iota(T.pat1[:], [[1, 2], [0, 4], [2, 16]], 0, 0, allow_small_or_imprecise_dtypes=True))
+    order = far + near
+    s_pb = stage()
+    a = 0
+    while a < 16:
+        b = a + 1
+        while b < 16 and order[b] == order[b - 1] + 1:
+            b += 1
+        done(g.iota(T.patb[:, a * 4:b * 4], [[1, (b - a) * 4]], order[a] * 4, 0, allow_small_or_imprecise_dtypes=True), s_pb)
+        a = b
+    s_v8 = one(g.iota(T.v8[:], [[-16, 8]], 0, 1))
+
+    need(V, s_d)
+    s_id = one(ts(T.ident[:], T.d128[:], 128.0, A.is_equal))
+    s_c1 = stage()
+    done(ts(T.lstr[:], T.d128[:], 128.0, A.is_gt), s_c1)
+    done(V.memset(T.ones[:], 1.0), s_c1)
+    need(V, s_kp)
+    s_rm = one(ts(T.rmask[:], T.kpat[:], 1.0, A.min))
+
+    IOWN, IA, IB, IM, ILO, IO4, IO64, ICNT, IK1, IT, IHB, IJX = range(12)
+    FOWN, FT1, FT3, FIB, FLO, FU, FHI, FK1, FK2, FV1, FXB, FVAL = range(12)
+    need(V, s_idx)
+    s_a = one(ts(iw(IOWN), T.idx_s[:], 13, A.arith_shift_right))
+    need(V, s_a)
+    s_b = one(V.tensor_copy(fw(FOWN), iw(IOWN)))
+    need(V, s_b, s_io)
+    s_e = stage()
+    for k in range(8):
+        done(ts(T.e2[:, k:128:8], T.io16[:], T.fw[:, FOWN * 8 + k:FOWN * 8 + k + 1], A.is_equal), s_e)
+    need(V, s_e, s_rm)
+    s_sc = one(V.tensor_tensor_scan(T.incl[:], T.rmask[:], T.e2[:], 0.0, A.mult, A.add))
+    need(V, s_sc)
+    s_ex = one(V.tensor_tensor(T.excl[:], T.incl[:], T.e2[:], A.subtract))
+
+    s_h1 = stage()
+    done(ts(iw(IA), T.idx_s[:], 1, A.bitwise_and), s_h1)
+    done(ts(iw(IB), T.idx_s[:], 1, A.arith_shift_right, 0xE00, A.bitwise_and), s_h1)
+    done(ts(iw(IM), T.idx_s[:], 1, A.arith_shift_right, 3, A.bitwise_and), s_h1)
+    done(ts(iw(ILO), T.idx_s[:], 3, A.arith_shift_right, 127, A.bitwise_and), s_h1)
+    done(ts(iw(IO4), T.idx_s[:], 11, A.arith_shift_right, 60, A.bitwise_and), s_h1)
+    done(ts(iw(IO64), T.idx_s[:], 7, A.arith_shift_right, 960, A.bitwise_and), s_h1)
+    need(V, s_h1)
+    s_h2 = stage()
+    done(ts(fw(FT1), iw(IA), 4096.0, A.mult), s_h2)
+    done(ts(fw(FT3), iw(IM), 128.0, A.mult), s_h2)
+    done(V.tensor_copy(fw(FIB), iw(IB)), s_h2)
+    done(V.tensor_copy(fw(FLO), iw(ILO)), s_h2)
+    need(V, s_h2)
+    s_h3 = one(V.tensor_tensor(fw(FU), fw(FT1), fw(FT3), A.add))
+    need(V, s_h3)
+    s_h4 = one(V.tensor_tensor(fw(FHI), fw(FU), fw(FIB), A.add))
+
+    s_tp = [stage() for _ in GROUPS]
+    s_cp = [stage() for _ in GROUPS]
+    t0s = [sum(GROUPS[:i]) for i in range(len(GROUPS))]
+    ld_seen = [False] * 8
+
+    def transposes(gi, lo, hi):
+        for i in range(lo, hi):
+            t = t0s[gi] + i
+            if not ld_seen[t // 4]:
+                need(PE, s_ld[t // 4])
+                ld_seen[t // 4] = True
+            done(PE.transpose(T.ps[:, GBANK[gi] * 512 + i * 128:GBANK[gi] * 512 + (i + 1) * 128],
+                              T.raw[:, t * 128:(t + 1) * 128], T.ident[:]), s_tp[gi])
+
+    def copies(gi):
+        n = GROUPS[gi] * 128
+        q = S if gi in ON_SCALAR else V
+        need(q, s_tp[gi])
+        for jj in range(2):
+            for h in range(2):
+                o = T.win[h * 64:(h + 1) * 64, jj * 4096 + t0s[gi] * 128:jj * 4096 + t0s[gi] * 128 + n]
+                i = T.ps[jj * 64:(jj + 1) * 64, GBANK[gi] * 512:GBANK[gi] * 512 + n]
+                if gi in ON_SCALAR:
+                    done(S.activation(o, i, ActivationFunctionType.Copy), s_cp[gi])
+                else:
+                    done(V.tensor_copy(o, i), s_cp[gi])
+
+    need(PE, s_id)
+    transposes(0, 0, 3)
+    need(PE, s_c1, s_e, s_ex)
+    s_cm = stage()
+    done(PE.matmul(bank(6, 128), T.lstr[:], T.e2[:], True, False), s_cm)
+    done(PE.matmul(bank(6, 128), T.ones[:], T.excl[:], False, True), s_cm)
+    transposes(0, 3, 4)
+
+    need(V, s_cm)
+    s_p = one(V.tensor_tensor(T.prod[:], bank(6, 128), T.e2[:], A.mult))
+    need(V, s_p)
+    s_t1 = one(V.tensor_tensor(T.tree[:, 0:64], T.prod[:, 0:64], T.prod[:, 64:128], A.add))
+    need(V, s_t1)
+    s_t2 = one(V.tensor_tensor(T.tree[:, 64:96], T.tree[:, 0:32], T.tree[:, 32:64], A.add))
+    need(V, s_t2)
+    s_t3 = one(V.tensor_tensor(T.tree[:, 96:112], T.tree[:, 64:80], T.tree[:, 80:96], A.add))
+    need(V, s_t3)
+    s_cn = one(V.tensor_tensor(iw(ICNT), T.tree[:, 96:104], T.tree[:, 104:112], A.add))
+    need(V, s_cn)
+    s_k1 = stage()
+    done(ts(iw(IK1), iw(ICNT), 31, A.bitwise_and), s_k1)
+    done(ts(iw(IT), iw(ICNT), 5, A.arith_shift_right), s_k1)
+    done(ts(iw(IHB), iw(ICNT), 1, A.bitwise_and), s_k1)
+    done(ts(iw(IJX), iw(ICNT), 1, A.arith_shift_right), s_k1)
+    need(V, s_k1)
+    s_k2 = stage()
+    done(V.tensor_copy(fw(FK1), iw(IK1)), s_k2)
+    done(V.tensor_tensor(fw(FK2), iw(IO4), iw(IT), A.add), s_k2)
+    need(V, s_k2, s_h4, s_p1, s_pb)
+    s_ab = stage()
+    for k in range(8):
+        def col(i):
+            return T.fw[:, i * 8 + k:i * 8 + k + 1]
+        done(ts(T.amat[:, k * 128:(k + 1) * 128], T.pat1[:], col(FK1), A.is_equal), s_ab)
+        done(ts(T.bhi[:, k * 64:(k + 1) * 64], T.patb[:], col(FK2), A.is_equal, col(FHI), A.mult), s_ab)
+        done(ts(T.blo[:, k * 64:(k + 1) * 64], T.patb[:], col(FK2), A.is_equal, col(FLO), A.mult), s_ab)
+
+    transposes(1, 0, 4)
+    transposes(2, 0, 4)
+    need(PE, s_ab)
+    s_rm2 = stage()
+    for k in range(8):
+        done(PE.matmul(bank(7, 64), T.amat[:, k * 128:(k + 1) * 128], T.bhi[:, k * 64:(k + 1) * 64], k == 0, False), s_rm2)
+        done(PE.matmul(bank(7, 64), T.amat[:, k * 128:(k + 1) * 128], T.blo[:, k * 64:(k + 1) * 64], False, k == 7), s_rm2)
+    need(V, s_rm2)
+    s_req = one(V.tensor_copy(T.req16[:], bank(7, 64)))
+
+    sent = 0
+    H = P["helpers"][P["peer"][me]]
+    wq = 32 // NF
+    need(g, s_req)
+    sent += _fused(g, core, topo, [(H[f], T.req16[:, f * wq:(f + 1) * wq], T.rqf[:], T.sem.fq) for f in range(NF)],
+                   8 // NF, T.sem.snt)
+    others = [o for o in near if o != me]
+    items = []
+    for o in others:
+        po = 8 + [x for x in P["near"][o] if x != o].index(me)
+        pq = 8 + near.index(o)
+        items.append((cores[o], T.req16[:, pq * 4:pq * 4 + 4], T.offs[:, po * 4:po * 4 + 4], T.sem.rqN))
+    sent += _fused(g, core, topo, items, 1, T.sem.snt)
+
+    s_k3 = stage()
+    done(V.tensor_tensor(fw(FV1), iw(IO64), iw(IJX), A.add), s_k3)
+    done(ts(T.fw[:, FXB * 8:FXB * 8 + 4], T.iw[:, IHB * 8:IHB * 8 + 4], 1024.0, A.mult), s_k3)
+    done(ts(T.fw[:, FXB * 8 + 4:FXB * 8 + 8], T.iw[:, IHB * 8 + 4:IHB * 8 + 8], -1024.0, A.mult, 1024.0, A.add), s_k3)
+    need(V, s_v8)
+    done(ts(T.v8s[:], T.v8[:], 4, A.arith_shift_right), s_k3)
+    done(ts(T.amod[:], T.d128[:], 15, A.bitwise_and), s_k3)
+    need(V, s_k3)
+    s_k4 = stage()
+    done(V.tensor_tensor(fw(FVAL), fw(FV1), fw(FXB), A.add), s_k4)
+    done(ts(T.mask8[:], T.v8s[:], 0.0, A.is_equal), s_k4)
+    s_a2 = stage()
+    done(ts(T.a2[:, 0:64], T.amod[:, 0:64], 0.0, A.is_equal), s_a2)
+    done(ts(T.a2[:, 192:256], T.amod[:, 64:128], 0.0, A.is_equal), s_a2)
+    done(V.memset(T.a2[:, 64:192], 0.0), s_a2)
+    need(V, s_k4)
+    s_rh = stage()
+    for k in range(8):
+        done(ts(T.rhsf[:, k * 8:(k + 1) * 8], T.mask8[:], T.fw[:, FVAL * 8 + k:FVAL * 8 + k + 1], A.mult), s_rh)
+
+    for gi in range(3):
+        copies(gi)
+    for gi in range(3, len(GROUPS)):
+        if gi == 6:
+            need(PE, s_p)
+        if gi == 7:
+            need(PE, s_req)
+        if gi >= 8:
+            need(PE, s_cp[gi - 8])
+        transposes(gi, 0, GROUPS[gi])
+        copies(gi)
+    need(PE, s_rh, s_a2, s_cp[3])
+    s_fo = stage()
+    done(PE.matmul(bank(3, 32), T.a2[:, 0:128], T.rhsf[:, 0:32], True, False), s_fo)
+    done(PE.matmul(bank(3, 32), T.a2[:, 128:256], T.rhsf[:, 32:64], False, True), s_fo)
+
+    need(V, *s_cp)
+    V.wait_ge(T.sem.rqF, 16)
+    s_gf = one(V.tensor_copy(T.outb[:, 0:512], T.win[:, 0:8192].indirect(T.offs[:, 0:32])))
+    V.wait_ge(T.sem.rqN, 7)
+    s_gn = one(V.tensor_copy(T.outb[:, 512:960], T.win[:, 0:8192].indirect(T.offs[:, 32:60])))
+    pown = 8 + near.index(me)
+    s_go = one(V.tensor_copy(T.land[:, me * 64:(me + 1) * 64],
+                             T.win[:, 0:8192].indirect(T.req16[:, pown * 4:pown * 4 + 4])))
+    wr = 512 // NF
+    need(g, s_gf)
+    sent += _fused(g, core, topo, [(H[f], T.outb[:, f * wr:(f + 1) * wr], T.rsf[:], T.sem.fr) for f in range(NF)],
+                   8 // NF, T.sem.snt)
+    need(g, s_gn)
+    sent += _fused(g, core, topo, [(cores[q], T.outb[:, (8 + i) * 64:(9 + i) * 64], T.land[:, me * 64:(me + 1) * 64],
+                                    T.sem.rsN) for i, q in enumerate(others)], 1, T.sem.snt)
+    need(V, s_fo)
+    s_ff = one(V.tensor_copy(T.foffs[:], bank(3, 32)))
+
+    def runs(lst):
+        out = []
+        for x in sorted(lst):
+            if out and out[-1][1] == x:
+                out[-1][1] = x + 1
+            else:
+                out.append([x, x + 1])
+        return out
+
+    s_du = stage()
+    for sem, cnt, lst in ((T.sem.rsN, 7, near), (T.sem.rsF, 16, far)):
+        V.wait_ge(sem, cnt)
+        S.wait_ge(sem, cnt)
+        need(V, s_go)
+        need(S, s_go)
+        for lo, hi in runs(lst):
+            done(V.tensor_copy(T.land[0:64, 1024 + lo * 64:1024 + hi * 64], T.land[64:128, lo * 64:hi * 64]), s_du)
+            done(S.activation(T.land[64:128, 1024 + lo * 64:1024 + hi * 64], T.land[0:64, lo * 64:hi * 64],
+                              ActivationFunctionType.Copy), s_du)
+    need(V, s_du, s_ff)
+    s_g = one(V.tensor_copy(T.gat[:], T.land[:, 0:2048].indirect(T.foffs[:, 0:32])))
+    need(PE, s_g)
+    s_st = stage()
+    for kk in range(4):
+        s_t = one(PE.transpose(bank(4 + kk, 128), T.gat[:, kk * 128:(kk + 1) * 128], T.ident[:]))
+        o = T.ysb[:, kk * 128:(kk + 1) * 128]
+        if kk % 2 == 0:
+            need(V, s_t)
+            s_y = one(V.tensor_copy(o, bank(4 + kk, 128)))
+            q = SY
+        else:
+            need(S, s_t)
+            s_y = one(S.activation(o, bank(4 + kk, 128), ActivationFunctionType.Copy))
+            q = S
+        need(q, s_y)
+        for hh in range(2):
+            r0 = (hh * 4 + kk) * 128
+            done(q.dma_start(T.y[r0:r0 + 128, :], T.ysb[:, kk * 128 + hh * 64:kk * 128 + hh * 64 + 64]), s_st, 16)
+
+    g.wait_ge(T.sem.snt, sent)
+    need(g, *stages)

@@ -3,53 +3,29 @@ from concourse.mybir import AluOpType, ActivationFunctionType
 
 NSIM = 512
 NF = 2
+REQ_AFTER = 2
 NPOOL = 120
 GROUPS = [4, 4, 4, 4, 4, 4, 3, 2, 1, 1, 1]
 GBANK = [0, 1, 2, 3, 4, 5, 6, 7, 0, 1, 2]
 ON_SCALAR = [0, 1, 2, 4, 6, 8, 10]
 
+
+def _sb(n, d="float32"):
+    return ("sbuf", [128, n], d)
+
+
 SCRATCH = {
-    "idx_s": ("sbuf", [128, 8], "int32"),
-    "raw": ("sbuf", [128, 4096], "float32"),
-    "win": ("sbuf", [128, 8192], "float32"),
-    "ident": ("sbuf", [128, 128], "float32"),
-    "d128": ("sbuf", [128, 128], "int32"),
-    "amod": ("sbuf", [128, 128], "int32"),
-    "a2": ("sbuf", [128, 256], "float32"),
-    "lstr": ("sbuf", [128, 128], "bfloat16"),
-    "ones": ("sbuf", [128, 128], "bfloat16"),
-    "io16": ("sbuf", [128, 16], "float32"),
-    "kpat": ("sbuf", [128, 128], "bfloat16"),
-    "rmask": ("sbuf", [128, 128], "bfloat16"),
-    "pat1": ("sbuf", [128, 128], "bfloat16"),
-    "patb": ("sbuf", [128, 64], "bfloat16"),
-    "v8": ("sbuf", [128, 8], "int32"),
-    "v8s": ("sbuf", [128, 8], "int32"),
-    "mask8": ("sbuf", [128, 8], "float32"),
-    "iw": ("sbuf", [128, 96], "int32"),
-    "fw": ("sbuf", [128, 104], "float32"),
-    "e2": ("sbuf", [128, 128], "bfloat16"),
-    "incl": ("sbuf", [128, 128], "bfloat16"),
-    "excl": ("sbuf", [128, 128], "bfloat16"),
-    "prod": ("sbuf", [128, 128], "float32"),
-    "tree": ("sbuf", [128, 112], "float32"),
-    "amat": ("sbuf", [128, 1024], "bfloat16"),
-    "bhi": ("sbuf", [128, 512], "bfloat16"),
-    "blo": ("sbuf", [128, 512], "bfloat16"),
-    "req16": ("sbuf", [128, 64], "uint16"),
-    "offs": ("sbuf", [128, 60], "uint16"),
-    "outb": ("sbuf", [128, 960], "float32"),
-    "land": ("sbuf", [128, 2048], "float32"),
-    "rhsf": ("sbuf", [128, 64], "float32"),
-    "foffs": ("sbuf", [128, 32], "uint16"),
-    "gat": ("sbuf", [128, 512], "float32"),
-    "ysb": ("sbuf", [128, 512], "float32"),
-    "rqf": ("sbuf", [128, 32 // NF], "uint16"),
-    "rsf": ("sbuf", [128, 512 // NF], "float32"),
-    "ps": ("psum", [128, 4096], "float32"),
+    "idx_s": _sb(8, "int32"), "raw": _sb(4096), "win": _sb(8192), "ident": _sb(128), "d128": _sb(128, "int32"),
+    "amod": _sb(128, "int32"), "a2": _sb(256), "lstr": _sb(128, "bfloat16"), "ones": _sb(128, "bfloat16"),
+    "io16": _sb(16), "kpat": _sb(128, "bfloat16"), "rmask": _sb(128, "bfloat16"), "pat1": _sb(128, "bfloat16"),
+    "patb": _sb(64, "bfloat16"), "v8": _sb(8, "int32"), "v8s": _sb(8, "int32"), "mask8": _sb(8),
+    "iw": _sb(96, "int32"), "fw": _sb(104), "e2": _sb(128, "bfloat16"), "incl": _sb(128, "bfloat16"),
+    "excl": _sb(128, "bfloat16"), "prod": _sb(128), "tree": _sb(112), "amat": _sb(1024, "bfloat16"),
+    "bhi": _sb(512, "bfloat16"), "blo": _sb(512, "bfloat16"), "req16": _sb(64, "uint16"), "offs": _sb(60, "uint16"),
+    "outb": _sb(960), "land": _sb(2048), "rhsf": _sb(64), "foffs": _sb(32, "uint16"), "gat": _sb(512), "ysb": _sb(512),
+    "rqf": _sb(32 // NF, "uint16"), "rsf": _sb(512 // NF), "ps": ("psum", [128, 4096], "float32"),
 }
 SEMAPHORES = ["rqF", "rqN", "rsF", "rsN", "fq", "fr", "snt"] + ["s%d" % i for i in range(NPOOL)]
-
 _CACHE = {}
 
 
@@ -59,29 +35,30 @@ def _plan(T, topo):
     cores = list(T.cores)
     n = len(cores)
     rk = [topo.rack(topo.host(c)) for c in cores]
-    far = [[d for d in range(n) if rk[d] != rk[r]] for r in range(n)]
+    far = [[d for d in range(n) if rk[d] != rk[r] and not topo.may_write(cores[r], cores[d])]
+           + [d for d in range(n) if rk[d] != rk[r] and topo.may_write(cores[r], cores[d])] for r in range(n)]
     near = [[d for d in range(n) if rk[d] == rk[r]] for r in range(n)]
     peer = [[d for d in far[r] if topo.may_write(cores[r], cores[d]) and topo.chip(cores[d]) == topo.chip(cores[r])][0]
             for r in range(n)]
-    helpers = []
-    fwd = {}
+    hf, hn, role = [], [], {}
     for r in range(n):
         c0 = cores[r]
-        hs = [c for c in range(NSIM) if topo.host(c) == topo.host(c0) and topo.chip(c) == topo.chip(c0)
-              and c != c0 and topo.die(c) != topo.die(c0)][:NF]
-        helpers.append(hs)
-        for f, c in enumerate(hs):
-            fwd[c] = (r, f)
-    p = {"cores": cores, "far": far, "near": near, "peer": peer, "helpers": helpers, "fwd": fwd}
+        chipc = [c for c in range(NSIM) if topo.host(c) == topo.host(c0) and topo.chip(c) == topo.chip(c0) and c != c0]
+        hf.append([c for c in chipc if topo.die(c) != topo.die(c0)][:NF])
+        hn.append([c for c in chipc if topo.die(c) == topo.die(c0)][:NF])
+        for f in range(NF):
+            role[hf[r][f]] = ("F", r, f)
+            role[hn[r][f]] = ("N", r, f)
+    p = {"cores": cores, "far": far, "near": near, "peer": peer, "hf": hf, "hn": hn, "role": role}
     _CACHE["p"] = p
     return p
 
 
-def _fused(g, core, topo, items, per, lsem):
+def _fused(g, core, topo, items, per, lsem, avoid=0):
     m = 0xFFFF
     for it in items:
         m &= topo.mask(core, it[0])
-    e = [1 << b for b in range(16) if (m >> b) & 1]
+    e = [1 << b for b in range(16) if (m >> b) & 1 and not (avoid >> b) & 1]
     trs = []
     for i, (d, s, o, rs) in enumerate(items):
         mk = 0
@@ -93,20 +70,32 @@ def _fused(g, core, topo, items, per, lsem):
     return per * len(items)
 
 
-def _forwarder(g, core, T, topo, P, x, f):
-    s = P["peer"][x]
+def _oth(P, r):
+    return [x for x in P["near"][r] if x != r]
+
+
+def _helper(g, core, T, topo, P, kind, x, f):
     cores = P["cores"]
-    nb = 8 // NF
-    dsts = P["far"][s][f * nb:(f + 1) * nb]
-    per = 8 // nb
-    sent = 0
-    g.wait_ge(T.sem.fq, 8 // NF)
-    sent += _fused(g, core, topo, [(cores[o], T.rqf[:, i * 4:(i + 1) * 4],
-                                    T.offs[:, P["far"][o].index(s) * 4:P["far"][o].index(s) * 4 + 4], T.sem.rqF)
-                                   for i, o in enumerate(dsts)], per, T.sem.snt)
-    g.wait_ge(T.sem.fr, 8 // NF)
-    sent += _fused(g, core, topo, [(cores[q], T.rsf[:, i * 64:(i + 1) * 64], T.land[:, s * 64:(s + 1) * 64], T.sem.rsF)
-                                   for i, q in enumerate(dsts)], per, T.sem.snt)
+    rq, rs = [], []
+    if kind == "F":
+        s = P["peer"][x]
+        for i, o in enumerate(P["far"][s][f * 4:(f + 1) * 4]):
+            po = P["far"][o].index(s)
+            rq.append((cores[o], T.rqf[:, i * 4:(i + 1) * 4], T.offs[:, po * 4:po * 4 + 4], T.sem.rqF))
+        for i, q in enumerate(P["far"][s][f * 2:(f + 1) * 2]):
+            rs.append((cores[q], T.rsf[:, i * 64:(i + 1) * 64], T.land[:, s * 64:(s + 1) * 64], T.sem.rsF))
+    else:
+        for i, o in enumerate(P["near"][x][f * 4:(f + 1) * 4]):
+            if o != x:
+                po = 8 + _oth(P, o).index(x)
+                rq.append((cores[o], T.rqf[:, i * 4:(i + 1) * 4], T.offs[:, po * 4:po * 4 + 4], T.sem.rqN))
+        for i in range(f, 4):
+            q = _oth(P, x)[3 * f + i]
+            rs.append((cores[q], T.rsf[:, i * 64:(i + 1) * 64], T.land[:, x * 64:(x + 1) * 64], T.sem.rsN))
+    g.wait_ge(T.sem.fq, 4)
+    sent = _fused(g, core, topo, rq, 2, T.sem.snt)
+    g.wait_ge(T.sem.fr, 4)
+    sent += _fused(g, core, topo, rs, 4 if kind == "F" else 2, T.sem.snt)
     g.wait_ge(T.sem.snt, sent)
 
 
@@ -114,10 +103,11 @@ def rank_program(g, core, T, topo):
     P = _plan(T, topo)
     me = T.rank_of(core)
     if me is None:
-        if core in P["fwd"]:
-            _forwarder(g, core, T, topo, P, P["fwd"][core][0], P["fwd"][core][1])
+        if core in P["role"]:
+            _helper(g, core, T, topo, P, *P["role"][core])
         return
     A = AluOpType
+    CP = ActivationFunctionType.Copy
     V, S, PE, SY = g.vector, g.scalar, g.tensor, g.sync
     cores, far, near = P["cores"], P["far"][me], P["near"][me]
     stages = []
@@ -144,6 +134,9 @@ def rank_program(g, core, T, topo):
         if op1 is None:
             return V.tensor_scalar(out, in0, s1, None, op0)
         return V.tensor_scalar(out, in0, s1, s2, op0, op1)
+
+    def tt(out, a, b, op):
+        return V.tensor_tensor(out, a, b, op)
 
     def iw(i):
         return T.iw[:, i * 8:(i + 1) * 8]
@@ -185,8 +178,9 @@ def rank_program(g, core, T, topo):
 
     IOWN, IA, IB, IM, ILO, IO4, IO64, ICNT, IK1, IT, IHB, IJX = range(12)
     FOWN, FT1, FT3, FIB, FLO, FU, FHI, FK1, FK2, FV1, FXB, FVAL = range(12)
+    SR, BA = A.arith_shift_right, A.bitwise_and
     need(V, s_idx)
-    s_a = one(ts(iw(IOWN), T.idx_s[:], 13, A.arith_shift_right))
+    s_a = one(ts(iw(IOWN), T.idx_s[:], 13, SR))
     need(V, s_a)
     s_b = one(V.tensor_copy(fw(FOWN), iw(IOWN)))
     need(V, s_b, s_io)
@@ -196,15 +190,15 @@ def rank_program(g, core, T, topo):
     need(V, s_e, s_rm)
     s_sc = one(V.tensor_tensor_scan(T.incl[:], T.rmask[:], T.e2[:], 0.0, A.mult, A.add))
     need(V, s_sc)
-    s_ex = one(V.tensor_tensor(T.excl[:], T.incl[:], T.e2[:], A.subtract))
+    s_ex = one(tt(T.excl[:], T.incl[:], T.e2[:], A.subtract))
 
     s_h1 = stage()
-    done(ts(iw(IA), T.idx_s[:], 1, A.bitwise_and), s_h1)
-    done(ts(iw(IB), T.idx_s[:], 1, A.arith_shift_right, 0xE00, A.bitwise_and), s_h1)
-    done(ts(iw(IM), T.idx_s[:], 1, A.arith_shift_right, 3, A.bitwise_and), s_h1)
-    done(ts(iw(ILO), T.idx_s[:], 3, A.arith_shift_right, 127, A.bitwise_and), s_h1)
-    done(ts(iw(IO4), T.idx_s[:], 11, A.arith_shift_right, 60, A.bitwise_and), s_h1)
-    done(ts(iw(IO64), T.idx_s[:], 7, A.arith_shift_right, 960, A.bitwise_and), s_h1)
+    done(ts(iw(IA), T.idx_s[:], 1, BA), s_h1)
+    done(ts(iw(IB), T.idx_s[:], 1, SR, 0xE00, BA), s_h1)
+    done(ts(iw(IM), T.idx_s[:], 1, SR, 3, BA), s_h1)
+    done(ts(iw(ILO), T.idx_s[:], 3, SR, 127, BA), s_h1)
+    done(ts(iw(IO4), T.idx_s[:], 11, SR, 60, BA), s_h1)
+    done(ts(iw(IO64), T.idx_s[:], 7, SR, 960, BA), s_h1)
     need(V, s_h1)
     s_h2 = stage()
     done(ts(fw(FT1), iw(IA), 4096.0, A.mult), s_h2)
@@ -212,9 +206,9 @@ def rank_program(g, core, T, topo):
     done(V.tensor_copy(fw(FIB), iw(IB)), s_h2)
     done(V.tensor_copy(fw(FLO), iw(ILO)), s_h2)
     need(V, s_h2)
-    s_h3 = one(V.tensor_tensor(fw(FU), fw(FT1), fw(FT3), A.add))
+    s_h3 = one(tt(fw(FU), fw(FT1), fw(FT3), A.add))
     need(V, s_h3)
-    s_h4 = one(V.tensor_tensor(fw(FHI), fw(FU), fw(FIB), A.add))
+    s_h4 = one(tt(fw(FHI), fw(FU), fw(FIB), A.add))
 
     s_tp = [stage() for _ in GROUPS]
     s_cp = [stage() for _ in GROUPS]
@@ -238,10 +232,7 @@ def rank_program(g, core, T, topo):
             for h in range(2):
                 o = T.win[h * 64:(h + 1) * 64, jj * 4096 + t0s[gi] * 128:jj * 4096 + t0s[gi] * 128 + n]
                 i = T.ps[jj * 64:(jj + 1) * 64, GBANK[gi] * 512:GBANK[gi] * 512 + n]
-                if gi in ON_SCALAR:
-                    done(S.activation(o, i, ActivationFunctionType.Copy), s_cp[gi])
-                else:
-                    done(V.tensor_copy(o, i), s_cp[gi])
+                done(S.activation(o, i, CP) if gi in ON_SCALAR else V.tensor_copy(o, i), s_cp[gi])
 
     need(PE, s_id)
     transposes(0, 0, 3)
@@ -252,25 +243,25 @@ def rank_program(g, core, T, topo):
     transposes(0, 3, 4)
 
     need(V, s_cm)
-    s_p = one(V.tensor_tensor(T.prod[:], bank(6, 128), T.e2[:], A.mult))
+    s_p = one(tt(T.prod[:], bank(6, 128), T.e2[:], A.mult))
     need(V, s_p)
-    s_t1 = one(V.tensor_tensor(T.tree[:, 0:64], T.prod[:, 0:64], T.prod[:, 64:128], A.add))
+    s_t1 = one(tt(T.tree[:, 0:64], T.prod[:, 0:64], T.prod[:, 64:128], A.add))
     need(V, s_t1)
-    s_t2 = one(V.tensor_tensor(T.tree[:, 64:96], T.tree[:, 0:32], T.tree[:, 32:64], A.add))
+    s_t2 = one(tt(T.tree[:, 64:96], T.tree[:, 0:32], T.tree[:, 32:64], A.add))
     need(V, s_t2)
-    s_t3 = one(V.tensor_tensor(T.tree[:, 96:112], T.tree[:, 64:80], T.tree[:, 80:96], A.add))
+    s_t3 = one(tt(T.tree[:, 96:112], T.tree[:, 64:80], T.tree[:, 80:96], A.add))
     need(V, s_t3)
-    s_cn = one(V.tensor_tensor(iw(ICNT), T.tree[:, 96:104], T.tree[:, 104:112], A.add))
+    s_cn = one(tt(iw(ICNT), T.tree[:, 96:104], T.tree[:, 104:112], A.add))
     need(V, s_cn)
     s_k1 = stage()
-    done(ts(iw(IK1), iw(ICNT), 31, A.bitwise_and), s_k1)
-    done(ts(iw(IT), iw(ICNT), 5, A.arith_shift_right), s_k1)
-    done(ts(iw(IHB), iw(ICNT), 1, A.bitwise_and), s_k1)
-    done(ts(iw(IJX), iw(ICNT), 1, A.arith_shift_right), s_k1)
+    done(ts(iw(IK1), iw(ICNT), 31, BA), s_k1)
+    done(ts(iw(IT), iw(ICNT), 5, SR), s_k1)
+    done(ts(iw(IHB), iw(ICNT), 1, BA), s_k1)
+    done(ts(iw(IJX), iw(ICNT), 1, SR), s_k1)
     need(V, s_k1)
     s_k2 = stage()
     done(V.tensor_copy(fw(FK1), iw(IK1)), s_k2)
-    done(V.tensor_tensor(fw(FK2), iw(IO4), iw(IT), A.add), s_k2)
+    done(tt(fw(FK2), iw(IO4), iw(IT), A.add), s_k2)
     need(V, s_k2, s_h4, s_p1, s_pb)
     s_ab = stage()
     for k in range(8):
@@ -280,8 +271,8 @@ def rank_program(g, core, T, topo):
         done(ts(T.bhi[:, k * 64:(k + 1) * 64], T.patb[:], col(FK2), A.is_equal, col(FHI), A.mult), s_ab)
         done(ts(T.blo[:, k * 64:(k + 1) * 64], T.patb[:], col(FK2), A.is_equal, col(FLO), A.mult), s_ab)
 
-    transposes(1, 0, 4)
-    transposes(2, 0, 4)
+    for gi in range(1, REQ_AFTER + 1):
+        transposes(gi, 0, 4)
     need(PE, s_ab)
     s_rm2 = stage()
     for k in range(8):
@@ -291,29 +282,25 @@ def rank_program(g, core, T, topo):
     s_req = one(V.tensor_copy(T.req16[:], bank(7, 64)))
 
     sent = 0
-    H = P["helpers"][P["peer"][me]]
-    wq = 32 // NF
+    HF = P["hf"][P["peer"][me]]
+    HN = P["hn"][me]
+    offchip = topo.mask(core, HF[0])
     need(g, s_req)
-    sent += _fused(g, core, topo, [(H[f], T.req16[:, f * wq:(f + 1) * wq], T.rqf[:], T.sem.fq) for f in range(NF)],
-                   8 // NF, T.sem.snt)
-    others = [o for o in near if o != me]
-    items = []
-    for o in others:
-        po = 8 + [x for x in P["near"][o] if x != o].index(me)
-        pq = 8 + near.index(o)
-        items.append((cores[o], T.req16[:, pq * 4:pq * 4 + 4], T.offs[:, po * 4:po * 4 + 4], T.sem.rqN))
-    sent += _fused(g, core, topo, items, 1, T.sem.snt)
+    sent += _fused(g, core, topo, [(HF[f], T.req16[:, f * 16:(f + 1) * 16], T.rqf[:], T.sem.fq) for f in range(NF)],
+                   4, T.sem.snt)
+    sent += _fused(g, core, topo, [(HN[f], T.req16[:, 32 + f * 16:48 + f * 16], T.rqf[:], T.sem.fq) for f in range(NF)],
+                   4, T.sem.snt, offchip)
 
     s_k3 = stage()
-    done(V.tensor_tensor(fw(FV1), iw(IO64), iw(IJX), A.add), s_k3)
+    done(tt(fw(FV1), iw(IO64), iw(IJX), A.add), s_k3)
     done(ts(T.fw[:, FXB * 8:FXB * 8 + 4], T.iw[:, IHB * 8:IHB * 8 + 4], 1024.0, A.mult), s_k3)
     done(ts(T.fw[:, FXB * 8 + 4:FXB * 8 + 8], T.iw[:, IHB * 8 + 4:IHB * 8 + 8], -1024.0, A.mult, 1024.0, A.add), s_k3)
     need(V, s_v8)
-    done(ts(T.v8s[:], T.v8[:], 4, A.arith_shift_right), s_k3)
-    done(ts(T.amod[:], T.d128[:], 15, A.bitwise_and), s_k3)
+    done(ts(T.v8s[:], T.v8[:], 4, SR), s_k3)
+    done(ts(T.amod[:], T.d128[:], 15, BA), s_k3)
     need(V, s_k3)
     s_k4 = stage()
-    done(V.tensor_tensor(fw(FVAL), fw(FV1), fw(FXB), A.add), s_k4)
+    done(tt(fw(FVAL), fw(FV1), fw(FXB), A.add), s_k4)
     done(ts(T.mask8[:], T.v8s[:], 0.0, A.is_equal), s_k4)
     s_a2 = stage()
     done(ts(T.a2[:, 0:64], T.amod[:, 0:64], 0.0, A.is_equal), s_a2)
@@ -324,16 +311,15 @@ def rank_program(g, core, T, topo):
     for k in range(8):
         done(ts(T.rhsf[:, k * 8:(k + 1) * 8], T.mask8[:], T.fw[:, FVAL * 8 + k:FVAL * 8 + k + 1], A.mult), s_rh)
 
-    for gi in range(3):
-        copies(gi)
-    for gi in range(3, len(GROUPS)):
-        if gi == 6:
-            need(PE, s_p)
-        if gi == 7:
-            need(PE, s_req)
-        if gi >= 8:
-            need(PE, s_cp[gi - 8])
-        transposes(gi, 0, GROUPS[gi])
+    for gi in range(len(GROUPS)):
+        if gi > REQ_AFTER:
+            if gi == 6:
+                need(PE, s_p)
+            if gi == 7:
+                need(PE, s_req)
+            if gi >= 8:
+                need(PE, s_cp[gi - 8])
+            transposes(gi, 0, GROUPS[gi])
         copies(gi)
     need(PE, s_rh, s_a2, s_cp[3])
     s_fo = stage()
@@ -343,18 +329,19 @@ def rank_program(g, core, T, topo):
     need(V, *s_cp)
     V.wait_ge(T.sem.rqF, 16)
     s_gf = one(V.tensor_copy(T.outb[:, 0:512], T.win[:, 0:8192].indirect(T.offs[:, 0:32])))
-    V.wait_ge(T.sem.rqN, 7)
+    V.wait_ge(T.sem.rqN, 14)
     s_gn = one(V.tensor_copy(T.outb[:, 512:960], T.win[:, 0:8192].indirect(T.offs[:, 32:60])))
     pown = 8 + near.index(me)
     s_go = one(V.tensor_copy(T.land[:, me * 64:(me + 1) * 64],
                              T.win[:, 0:8192].indirect(T.req16[:, pown * 4:pown * 4 + 4])))
-    wr = 512 // NF
     need(g, s_gf)
-    sent += _fused(g, core, topo, [(H[f], T.outb[:, f * wr:(f + 1) * wr], T.rsf[:], T.sem.fr) for f in range(NF)],
-                   8 // NF, T.sem.snt)
+    sent += _fused(g, core, topo, [(HF[f], T.outb[:, f * 128:(f + 1) * 128], T.rsf[:, 0:128], T.sem.fr) for f in range(NF)],
+                   4, T.sem.snt)
     need(g, s_gn)
-    sent += _fused(g, core, topo, [(cores[q], T.outb[:, (8 + i) * 64:(9 + i) * 64], T.land[:, me * 64:(me + 1) * 64],
-                                    T.sem.rsN) for i, q in enumerate(others)], 1, T.sem.snt)
+    sent += _fused(g, core, topo, [(HN[f], T.outb[:, 512 + f * 192:768 + f * 192], T.rsf[:], T.sem.fr) for f in range(NF)],
+                   4, T.sem.snt, offchip)
+    sent += _fused(g, core, topo, [(cores[q], T.outb[:, (4 + i) * 64:(5 + i) * 64], T.land[:, me * 64:(me + 1) * 64],
+                                    T.sem.rsF) for i, q in enumerate(far[4:8])], 2, T.sem.snt)
     need(V, s_fo)
     s_ff = one(V.tensor_copy(T.foffs[:], bank(3, 32)))
 
@@ -368,20 +355,20 @@ def rank_program(g, core, T, topo):
         return out
 
     s_du = stage()
-    for sem, cnt, lst in ((T.sem.rsN, 7, near), (T.sem.rsF, 16, far)):
+    for sem, cnt, lst in ((T.sem.rsN, 14, near), (T.sem.rsF, 24, far)):
         V.wait_ge(sem, cnt)
         S.wait_ge(sem, cnt)
         need(V, s_go)
         need(S, s_go)
         for lo, hi in runs(lst):
             done(V.tensor_copy(T.land[0:64, 1024 + lo * 64:1024 + hi * 64], T.land[64:128, lo * 64:hi * 64]), s_du)
-            done(S.activation(T.land[64:128, 1024 + lo * 64:1024 + hi * 64], T.land[0:64, lo * 64:hi * 64],
-                              ActivationFunctionType.Copy), s_du)
+            done(S.activation(T.land[64:128, 1024 + lo * 64:1024 + hi * 64], T.land[0:64, lo * 64:hi * 64], CP), s_du)
     need(V, s_du, s_ff)
-    s_g = one(V.tensor_copy(T.gat[:], T.land[:, 0:2048].indirect(T.foffs[:, 0:32])))
-    need(PE, s_g)
+    s_g = [one(V.tensor_copy(T.gat[:, kk * 128:(kk + 1) * 128],
+                             T.land[:, 0:2048].indirect(T.foffs[:, kk * 8:(kk + 1) * 8]))) for kk in range(4)]
     s_st = stage()
     for kk in range(4):
+        need(PE, s_g[kk])
         s_t = one(PE.transpose(bank(4 + kk, 128), T.gat[:, kk * 128:(kk + 1) * 128], T.ident[:]))
         o = T.ysb[:, kk * 128:(kk + 1) * 128]
         if kk % 2 == 0:
@@ -390,7 +377,7 @@ def rank_program(g, core, T, topo):
             q = SY
         else:
             need(S, s_t)
-            s_y = one(S.activation(o, bank(4 + kk, 128), ActivationFunctionType.Copy))
+            s_y = one(S.activation(o, bank(4 + kk, 128), CP))
             q = S
         need(q, s_y)
         for hh in range(2):

@@ -3,11 +3,11 @@ from concourse.mybir import AluOpType, ActivationFunctionType
 
 NSIM = 512
 NF = 2
-REQ_AFTER = 2
 NPOOL = 120
+AHEAD = 4
 GROUPS = [4, 4, 4, 4, 4, 4, 3, 2, 1, 1, 1]
 GBANK = [0, 1, 2, 3, 4, 5, 6, 7, 0, 1, 2]
-ON_SCALAR = [0, 1, 2, 4, 6, 8, 10]
+ON_SCALAR = [1, 3, 5, 7, 9]
 
 
 def _sb(n, d="float32"):
@@ -18,14 +18,14 @@ SCRATCH = {
     "idx_s": _sb(8, "int32"), "raw": _sb(4096), "win": _sb(8192), "ident": _sb(128), "d128": _sb(128, "int32"),
     "amod": _sb(128, "int32"), "a2": _sb(256), "lstr": _sb(128, "bfloat16"), "ones": _sb(128, "bfloat16"),
     "io16": _sb(16), "kpat": _sb(128, "bfloat16"), "rmask": _sb(128, "bfloat16"), "pat1": _sb(128, "bfloat16"),
-    "patb": _sb(64, "bfloat16"), "v8": _sb(8, "int32"), "v8s": _sb(8, "int32"), "mask8": _sb(8),
+    "patb": _sb(16, "bfloat16"), "v8": _sb(8, "int32"), "v8s": _sb(8, "int32"), "mask8": _sb(8),
     "iw": _sb(96, "int32"), "fw": _sb(104), "e2": _sb(128, "bfloat16"), "incl": _sb(128, "bfloat16"),
     "excl": _sb(128, "bfloat16"), "prod": _sb(128), "tree": _sb(112), "amat": _sb(1024, "bfloat16"),
-    "bhi": _sb(512, "bfloat16"), "blo": _sb(512, "bfloat16"), "req16": _sb(64, "uint16"), "offs": _sb(60, "uint16"),
+    "bhi": _sb(128, "bfloat16"), "blo": _sb(128, "bfloat16"), "req16": _sb(16, "uint16"), "offs": _sb(64, "uint16"),
     "outb": _sb(960), "land": _sb(2048), "rhsf": _sb(64), "foffs": _sb(32, "uint16"), "gat": _sb(512), "ysb": _sb(512),
-    "rqf": _sb(32 // NF, "uint16"), "rsf": _sb(512 // NF), "ps": ("psum", [128, 4096], "float32"),
+    "rsf": _sb(512 // NF), "ps": ("psum", [128, 4096], "float32"),
 }
-SEMAPHORES = ["rqF", "rqN", "rsF", "rsN", "fq", "fr", "snt"] + ["s%d" % i for i in range(NPOOL)]
+SEMAPHORES = ["rqF", "rqN", "rqO", "rsF", "rsC", "rsN", "fq", "fr", "snt", "sid"] + ["s%d" % i for i in range(NPOOL)]
 _CACHE = {}
 
 
@@ -74,42 +74,7 @@ def _oth(P, r):
     return [x for x in P["near"][r] if x != r]
 
 
-def _helper(g, core, T, topo, P, kind, x, f):
-    cores = P["cores"]
-    rq, rs = [], []
-    if kind == "F":
-        s = P["peer"][x]
-        for i, o in enumerate(P["far"][s][f * 4:(f + 1) * 4]):
-            po = P["far"][o].index(s)
-            rq.append((cores[o], T.rqf[:, i * 4:(i + 1) * 4], T.offs[:, po * 4:po * 4 + 4], T.sem.rqF))
-        for i, q in enumerate(P["far"][s][f * 2:(f + 1) * 2]):
-            rs.append((cores[q], T.rsf[:, i * 64:(i + 1) * 64], T.land[:, s * 64:(s + 1) * 64], T.sem.rsF))
-    else:
-        for i, o in enumerate(P["near"][x][f * 4:(f + 1) * 4]):
-            if o != x:
-                po = 8 + _oth(P, o).index(x)
-                rq.append((cores[o], T.rqf[:, i * 4:(i + 1) * 4], T.offs[:, po * 4:po * 4 + 4], T.sem.rqN))
-        for i in range(f, 4):
-            q = _oth(P, x)[3 * f + i]
-            rs.append((cores[q], T.rsf[:, i * 64:(i + 1) * 64], T.land[:, x * 64:(x + 1) * 64], T.sem.rsN))
-    g.wait_ge(T.sem.fq, 4)
-    sent = _fused(g, core, topo, rq, 2, T.sem.snt)
-    g.wait_ge(T.sem.fr, 4)
-    sent += _fused(g, core, topo, rs, 4 if kind == "F" else 2, T.sem.snt)
-    g.wait_ge(T.sem.snt, sent)
-
-
-def rank_program(g, core, T, topo):
-    P = _plan(T, topo)
-    me = T.rank_of(core)
-    if me is None:
-        if core in P["role"]:
-            _helper(g, core, T, topo, P, *P["role"][core])
-        return
-    A = AluOpType
-    CP = ActivationFunctionType.Copy
-    V, S, PE, SY = g.vector, g.scalar, g.tensor, g.sync
-    cores, far, near = P["cores"], P["far"][me], P["near"][me]
+def _kit(T):
     stages = []
 
     def stage():
@@ -130,6 +95,15 @@ def rank_program(g, core, T, topo):
         done(ins, s, n)
         return s
 
+    return stages, stage, done, need, one
+
+
+def _lists(g, T, kit, owners, want_f):
+    stages, stage, done, need, one = kit
+    A = AluOpType
+    V, PE = g.vector, g.tensor
+    nw = 4 * len(owners)
+
     def ts(out, in0, s1, op0, s2=None, op1=None):
         if op1 is None:
             return V.tensor_scalar(out, in0, s1, None, op0)
@@ -147,29 +121,21 @@ def rank_program(g, core, T, topo):
     def bank(b, n):
         return T.ps[:, b * 512:b * 512 + n]
 
-    s_idx = one(SY.dma_start(T.idx_s[:], T.idx[:]), 16)
-    s_ld = []
-    for b in range(8):
-        q = SY if b % 2 == 0 else S
-        s_ld.append(one(q.dma_start(T.raw[:, b * 512:(b + 1) * 512], T.tab[b * 1024:(b + 1) * 1024, :]), 16))
-
     s_d = one(g.iota(T.d128[:], [[1, 128]], 128, -1))
     s_io = one(g.iota(T.io16[:], [[1, 16]], 0, 0, allow_small_or_imprecise_dtypes=True))
     s_kp = one(g.iota(T.kpat[:], [[0, 16], [1, 8]], 0, 0, allow_small_or_imprecise_dtypes=True))
     s_p1 = one(g.iota(T.pat1[:], [[1, 2], [0, 4], [2, 16]], 0, 0, allow_small_or_imprecise_dtypes=True))
-    order = far + near
     s_pb = stage()
     a = 0
-    while a < 16:
+    while a < len(owners):
         b = a + 1
-        while b < 16 and order[b] == order[b - 1] + 1:
+        while b < len(owners) and owners[b] == owners[b - 1] + 1:
             b += 1
-        done(g.iota(T.patb[:, a * 4:b * 4], [[1, (b - a) * 4]], order[a] * 4, 0, allow_small_or_imprecise_dtypes=True), s_pb)
+        done(g.iota(T.patb[:, a * 4:b * 4], [[1, (b - a) * 4]], owners[a] * 4, 0, allow_small_or_imprecise_dtypes=True), s_pb)
         a = b
-    s_v8 = one(g.iota(T.v8[:], [[-16, 8]], 0, 1))
+    s_v8 = one(g.iota(T.v8[:], [[-16, 8]], 0, 1)) if want_f else None
 
     need(V, s_d)
-    s_id = one(ts(T.ident[:], T.d128[:], 128.0, A.is_equal))
     s_c1 = stage()
     done(ts(T.lstr[:], T.d128[:], 128.0, A.is_gt), s_c1)
     done(V.memset(T.ones[:], 1.0), s_c1)
@@ -179,7 +145,7 @@ def rank_program(g, core, T, topo):
     IOWN, IA, IB, IM, ILO, IO4, IO64, ICNT, IK1, IT, IHB, IJX = range(12)
     FOWN, FT1, FT3, FIB, FLO, FU, FHI, FK1, FK2, FV1, FXB, FVAL = range(12)
     SR, BA = A.arith_shift_right, A.bitwise_and
-    need(V, s_idx)
+    V.wait_ge(T.sem.fq, 4)
     s_a = one(ts(iw(IOWN), T.idx_s[:], 13, SR))
     need(V, s_a)
     s_b = one(V.tensor_copy(fw(FOWN), iw(IOWN)))
@@ -191,6 +157,11 @@ def rank_program(g, core, T, topo):
     s_sc = one(V.tensor_tensor_scan(T.incl[:], T.rmask[:], T.e2[:], 0.0, A.mult, A.add))
     need(V, s_sc)
     s_ex = one(tt(T.excl[:], T.incl[:], T.e2[:], A.subtract))
+
+    need(PE, s_c1, s_e, s_ex)
+    s_cm = stage()
+    done(PE.matmul(bank(6, 128), T.lstr[:], T.e2[:], True, False), s_cm)
+    done(PE.matmul(bank(6, 128), T.ones[:], T.excl[:], False, True), s_cm)
 
     s_h1 = stage()
     done(ts(iw(IA), T.idx_s[:], 1, BA), s_h1)
@@ -209,38 +180,6 @@ def rank_program(g, core, T, topo):
     s_h3 = one(tt(fw(FU), fw(FT1), fw(FT3), A.add))
     need(V, s_h3)
     s_h4 = one(tt(fw(FHI), fw(FU), fw(FIB), A.add))
-
-    s_tp = [stage() for _ in GROUPS]
-    s_cp = [stage() for _ in GROUPS]
-    t0s = [sum(GROUPS[:i]) for i in range(len(GROUPS))]
-    ld_seen = [False] * 8
-
-    def transposes(gi, lo, hi):
-        for i in range(lo, hi):
-            t = t0s[gi] + i
-            if not ld_seen[t // 4]:
-                need(PE, s_ld[t // 4])
-                ld_seen[t // 4] = True
-            done(PE.transpose(T.ps[:, GBANK[gi] * 512 + i * 128:GBANK[gi] * 512 + (i + 1) * 128],
-                              T.raw[:, t * 128:(t + 1) * 128], T.ident[:]), s_tp[gi])
-
-    def copies(gi):
-        n = GROUPS[gi] * 128
-        q = S if gi in ON_SCALAR else V
-        need(q, s_tp[gi])
-        for jj in range(2):
-            for h in range(2):
-                o = T.win[h * 64:(h + 1) * 64, jj * 4096 + t0s[gi] * 128:jj * 4096 + t0s[gi] * 128 + n]
-                i = T.ps[jj * 64:(jj + 1) * 64, GBANK[gi] * 512:GBANK[gi] * 512 + n]
-                done(S.activation(o, i, CP) if gi in ON_SCALAR else V.tensor_copy(o, i), s_cp[gi])
-
-    need(PE, s_id)
-    transposes(0, 0, 3)
-    need(PE, s_c1, s_e, s_ex)
-    s_cm = stage()
-    done(PE.matmul(bank(6, 128), T.lstr[:], T.e2[:], True, False), s_cm)
-    done(PE.matmul(bank(6, 128), T.ones[:], T.excl[:], False, True), s_cm)
-    transposes(0, 3, 4)
 
     need(V, s_cm)
     s_p = one(tt(T.prod[:], bank(6, 128), T.e2[:], A.mult))
@@ -268,28 +207,18 @@ def rank_program(g, core, T, topo):
         def col(i):
             return T.fw[:, i * 8 + k:i * 8 + k + 1]
         done(ts(T.amat[:, k * 128:(k + 1) * 128], T.pat1[:], col(FK1), A.is_equal), s_ab)
-        done(ts(T.bhi[:, k * 64:(k + 1) * 64], T.patb[:], col(FK2), A.is_equal, col(FHI), A.mult), s_ab)
-        done(ts(T.blo[:, k * 64:(k + 1) * 64], T.patb[:], col(FK2), A.is_equal, col(FLO), A.mult), s_ab)
+        done(ts(T.bhi[:, k * nw:(k + 1) * nw], T.patb[:, 0:nw], col(FK2), A.is_equal, col(FHI), A.mult), s_ab)
+        done(ts(T.blo[:, k * nw:(k + 1) * nw], T.patb[:, 0:nw], col(FK2), A.is_equal, col(FLO), A.mult), s_ab)
 
-    for gi in range(1, REQ_AFTER + 1):
-        transposes(gi, 0, 4)
     need(PE, s_ab)
     s_rm2 = stage()
     for k in range(8):
-        done(PE.matmul(bank(7, 64), T.amat[:, k * 128:(k + 1) * 128], T.bhi[:, k * 64:(k + 1) * 64], k == 0, False), s_rm2)
-        done(PE.matmul(bank(7, 64), T.amat[:, k * 128:(k + 1) * 128], T.blo[:, k * 64:(k + 1) * 64], False, k == 7), s_rm2)
+        done(PE.matmul(bank(7, nw), T.amat[:, k * 128:(k + 1) * 128], T.bhi[:, k * nw:(k + 1) * nw], k == 0, False), s_rm2)
+        done(PE.matmul(bank(7, nw), T.amat[:, k * 128:(k + 1) * 128], T.blo[:, k * nw:(k + 1) * nw], False, k == 7), s_rm2)
     need(V, s_rm2)
-    s_req = one(V.tensor_copy(T.req16[:], bank(7, 64)))
-
-    sent = 0
-    HF = P["hf"][P["peer"][me]]
-    HN = P["hn"][me]
-    offchip = topo.mask(core, HF[0])
-    need(g, s_req)
-    sent += _fused(g, core, topo, [(HF[f], T.req16[:, f * 16:(f + 1) * 16], T.rqf[:], T.sem.fq) for f in range(NF)],
-                   4, T.sem.snt)
-    sent += _fused(g, core, topo, [(HN[f], T.req16[:, 32 + f * 16:48 + f * 16], T.rqf[:], T.sem.fq) for f in range(NF)],
-                   4, T.sem.snt, offchip)
+    s_req = one(V.tensor_copy(T.req16[:, 0:nw], bank(7, nw)))
+    if not want_f:
+        return s_req, None
 
     s_k3 = stage()
     done(tt(fw(FV1), iw(IO64), iw(IJX), A.add), s_k3)
@@ -310,40 +239,135 @@ def rank_program(g, core, T, topo):
     s_rh = stage()
     for k in range(8):
         done(ts(T.rhsf[:, k * 8:(k + 1) * 8], T.mask8[:], T.fw[:, FVAL * 8 + k:FVAL * 8 + k + 1], A.mult), s_rh)
-
-    for gi in range(len(GROUPS)):
-        if gi > REQ_AFTER:
-            if gi == 6:
-                need(PE, s_p)
-            if gi == 7:
-                need(PE, s_req)
-            if gi >= 8:
-                need(PE, s_cp[gi - 8])
-            transposes(gi, 0, GROUPS[gi])
-        copies(gi)
-    need(PE, s_rh, s_a2, s_cp[3])
+    need(PE, s_rh, s_a2)
     s_fo = stage()
     done(PE.matmul(bank(3, 32), T.a2[:, 0:128], T.rhsf[:, 0:32], True, False), s_fo)
     done(PE.matmul(bank(3, 32), T.a2[:, 128:256], T.rhsf[:, 32:64], False, True), s_fo)
+    need(V, s_fo)
+    s_ff = one(V.tensor_copy(T.foffs[:], bank(3, 32)))
+    return s_req, s_ff
+
+
+def _helper(g, core, T, topo, P, kind, x, f):
+    cores = P["cores"]
+    kit = _kit(T)
+    stages, need = kit[0], kit[3]
+    rq, rs = [], []
+    if kind == "F":
+        s = P["peer"][x]
+        owners = P["far"][s][f * 4:(f + 1) * 4]
+        for i, o in enumerate(owners):
+            po = P["far"][o].index(s)
+            rq.append((cores[o], T.req16[:, i * 4:(i + 1) * 4], T.offs[:, po * 4:po * 4 + 4], T.sem.rqF))
+        for i, q in enumerate(P["far"][s][f * 2:(f + 1) * 2]):
+            rs.append((cores[q], T.rsf[:, i * 64:(i + 1) * 64], T.land[:, s * 64:(s + 1) * 64], T.sem.rsF))
+    else:
+        owners = P["near"][x][f * 4:(f + 1) * 4]
+        for i, o in enumerate(owners):
+            po = 15 if o == x else 8 + _oth(P, o).index(x)
+            rq.append((cores[o], T.req16[:, i * 4:(i + 1) * 4], T.offs[:, po * 4:po * 4 + 4], T.sem.rqN))
+        for i in range(f, 4):
+            q = _oth(P, x)[3 * f + i]
+            rs.append((cores[q], T.rsf[:, i * 64:(i + 1) * 64], T.land[:, x * 64:(x + 1) * 64], T.sem.rsN))
+    want_f = kind == "N" and f == NF - 1
+    s_req, s_ff = _lists(g, T, kit, owners, want_f)
+    g.wait_ge(T.sem.fq, 4)
+    need(g, s_req)
+    sent = _fused(g, core, topo, rq, 2, T.sem.snt)
+    if want_f:
+        need(g, s_ff)
+        sent += _fused(g, core, topo, [(cores[x], T.foffs[:], T.foffs[:], T.sem.rqO)], 4, T.sem.snt)
+    g.wait_ge(T.sem.fr, 4)
+    sent += _fused(g, core, topo, rs, 4 if kind == "F" else 2, T.sem.snt)
+    g.wait_ge(T.sem.snt, sent)
+    need(g, *stages)
+
+
+def rank_program(g, core, T, topo):
+    P = _plan(T, topo)
+    me = T.rank_of(core)
+    if me is None:
+        if core in P["role"]:
+            _helper(g, core, T, topo, P, *P["role"][core])
+        return
+    A = AluOpType
+    CP = ActivationFunctionType.Copy
+    V, S, PE, SY = g.vector, g.scalar, g.tensor, g.sync
+    cores, far, near = P["cores"], P["far"][me], P["near"][me]
+    stages, stage, done, need, one = _kit(T)
+
+    def bank(b, n):
+        return T.ps[:, b * 512:b * 512 + n]
+
+    s_idx = one(SY.dma_start(T.idx_s[:], T.idx[:]), 16)
+    s_ld = []
+    for b in range(8):
+        q = S if b < AHEAD and b % 2 == 1 else SY
+        if b == AHEAD:
+            SY.wait_ge(T.sem.sid, 16)
+        s_ld.append(one(q.dma_start(T.raw[:, b * 512:(b + 1) * 512], T.tab[b * 1024:(b + 1) * 1024, :]), 16))
+
+    s_d = one(g.iota(T.d128[:], [[1, 128]], 128, -1))
+    need(V, s_d)
+    s_id = one(V.tensor_scalar(T.ident[:], T.d128[:], 128.0, None, A.is_equal))
+
+    sent = 0
+    HF = P["hf"][P["peer"][me]]
+    HN = P["hn"][me]
+    offchip = topo.mask(core, HF[0])
+    need(g, s_idx)
+    _fused(g, core, topo, [(HF[f], T.idx_s[:], T.idx_s[:], T.sem.fq) for f in range(NF)], 4, T.sem.sid)
+    _fused(g, core, topo, [(HN[f], T.idx_s[:], T.idx_s[:], T.sem.fq) for f in range(NF)], 4, T.sem.sid, offchip)
+
+    s_tp = [stage() for _ in GROUPS]
+    s_cp = [stage() for _ in GROUPS]
+    t0s = [sum(GROUPS[:i]) for i in range(len(GROUPS))]
+    ld_seen = [False] * 8
+
+    def transposes(gi, lo, hi):
+        for i in range(lo, hi):
+            t = t0s[gi] + i
+            if not ld_seen[t // 4]:
+                need(PE, s_ld[t // 4])
+                ld_seen[t // 4] = True
+            done(PE.transpose(T.ps[:, GBANK[gi] * 512 + i * 128:GBANK[gi] * 512 + (i + 1) * 128],
+                              T.raw[:, t * 128:(t + 1) * 128], T.ident[:]), s_tp[gi])
+
+    def copies(gi):
+        n = GROUPS[gi] * 128
+        q = S if gi in ON_SCALAR else V
+        need(q, s_tp[gi])
+        for jj in range(2):
+            for h in range(2):
+                o = T.win[h * 64:(h + 1) * 64, jj * 4096 + t0s[gi] * 128:jj * 4096 + t0s[gi] * 128 + n]
+                i = T.ps[jj * 64:(jj + 1) * 64, GBANK[gi] * 512:GBANK[gi] * 512 + n]
+                done(S.activation(o, i, CP) if gi in ON_SCALAR else V.tensor_copy(o, i), s_cp[gi])
+
+    need(PE, s_id)
+    for gi in range(len(GROUPS)):
+        if gi >= 8:
+            need(PE, s_cp[gi - 8])
+        transposes(gi, 0, GROUPS[gi])
+        copies(gi)
 
     need(V, *s_cp)
     V.wait_ge(T.sem.rqF, 16)
-    s_gf = one(V.tensor_copy(T.outb[:, 0:512], T.win[:, 0:8192].indirect(T.offs[:, 0:32])))
-    V.wait_ge(T.sem.rqN, 14)
-    s_gn = one(V.tensor_copy(T.outb[:, 512:960], T.win[:, 0:8192].indirect(T.offs[:, 32:60])))
-    pown = 8 + near.index(me)
-    s_go = one(V.tensor_copy(T.land[:, me * 64:(me + 1) * 64],
-                             T.win[:, 0:8192].indirect(T.req16[:, pown * 4:pown * 4 + 4])))
-    need(g, s_gf)
+    s_gd = one(V.tensor_copy(T.outb[:, 0:256], T.win[:, 0:8192].indirect(T.offs[:, 0:16])))
+    s_gc = one(V.tensor_copy(T.outb[:, 256:512], T.win[:, 0:8192].indirect(T.offs[:, 16:32])))
+    need(S, *s_cp)
+    S.wait_ge(T.sem.rqN, 16)
+    s_gn = one(S.activation(T.outb[:, 512:960], T.win[:, 0:8192].indirect(T.offs[:, 32:60]), CP))
+    V.wait_ge(T.sem.rqN, 16)
+    s_go = one(V.tensor_copy(T.land[:, me * 64:(me + 1) * 64], T.win[:, 0:8192].indirect(T.offs[:, 60:64])))
+    need(g, s_gd)
     sent += _fused(g, core, topo, [(HF[f], T.outb[:, f * 128:(f + 1) * 128], T.rsf[:, 0:128], T.sem.fr) for f in range(NF)],
                    4, T.sem.snt)
     need(g, s_gn)
     sent += _fused(g, core, topo, [(HN[f], T.outb[:, 512 + f * 192:768 + f * 192], T.rsf[:], T.sem.fr) for f in range(NF)],
                    4, T.sem.snt, offchip)
+    need(g, s_gc)
     sent += _fused(g, core, topo, [(cores[q], T.outb[:, (4 + i) * 64:(5 + i) * 64], T.land[:, me * 64:(me + 1) * 64],
-                                    T.sem.rsF) for i, q in enumerate(far[4:8])], 2, T.sem.snt)
-    need(V, s_fo)
-    s_ff = one(V.tensor_copy(T.foffs[:], bank(3, 32)))
+                                    T.sem.rsC) for i, q in enumerate(far[4:8])], 2, T.sem.snt)
 
     def runs(lst):
         out = []
@@ -355,15 +379,16 @@ def rank_program(g, core, T, topo):
         return out
 
     s_du = stage()
-    for sem, cnt, lst in ((T.sem.rsN, 14, near), (T.sem.rsF, 24, far)):
+    need(V, s_go)
+    need(S, s_go)
+    for sem, cnt, lst in ((T.sem.rsN, 14, near), (T.sem.rsC, 8, far[4:8]), (T.sem.rsF, 16, far[0:4])):
         V.wait_ge(sem, cnt)
         S.wait_ge(sem, cnt)
-        need(V, s_go)
-        need(S, s_go)
         for lo, hi in runs(lst):
             done(V.tensor_copy(T.land[0:64, 1024 + lo * 64:1024 + hi * 64], T.land[64:128, lo * 64:hi * 64]), s_du)
             done(S.activation(T.land[64:128, 1024 + lo * 64:1024 + hi * 64], T.land[0:64, lo * 64:hi * 64], CP), s_du)
-    need(V, s_du, s_ff)
+    need(V, s_du)
+    V.wait_ge(T.sem.rqO, 4)
     s_g = [one(V.tensor_copy(T.gat[:, kk * 128:(kk + 1) * 128],
                              T.land[:, 0:2048].indirect(T.foffs[:, kk * 8:(kk + 1) * 8]))) for kk in range(4)]
     s_st = stage()
@@ -384,5 +409,6 @@ def rank_program(g, core, T, topo):
             r0 = (hh * 4 + kk) * 128
             done(q.dma_start(T.y[r0:r0 + 128, :], T.ysb[:, kk * 128 + hh * 64:kk * 128 + hh * 64 + 64]), s_st, 16)
 
+    g.wait_ge(T.sem.sid, 16)
     g.wait_ge(T.sem.snt, sent)
     need(g, *stages)

from concourse.bass import DstId, RemoteDMATransfer
from concourse.mybir import AluOpType, ActivationFunctionType

NSIM = 512
NF = 2
NPOOL = 120
AHEAD = 4
GROUPS = [4, 4, 4, 4, 4, 4, 3, 2, 1, 1, 1]
GBANK = [0, 1, 2, 3, 4, 5, 6, 7, 0, 1, 2]
ON_SCALAR = [1, 3, 5, 7, 9]


def _sb(n, d="float32"):
    return ("sbuf", [128, n], d)


SCRATCH = {
    "idx_s": _sb(8, "int32"), "raw": _sb(4096), "win": _sb(8192), "ident": _sb(128), "d128": _sb(128, "int32"),
    "amod": _sb(128, "int32"), "a2": _sb(256), "lstr": _sb(128, "bfloat16"), "ones": _sb(128, "bfloat16"),
    "io16": _sb(16), "kpat": _sb(128, "bfloat16"), "rmask": _sb(128, "bfloat16"), "pat1": _sb(128, "bfloat16"),
    "patb": _sb(16, "bfloat16"), "v8": _sb(8, "int32"), "v8s": _sb(8, "int32"), "mask8": _sb(8),
    "iw": _sb(96, "int32"), "fw": _sb(104), "e2": _sb(128, "bfloat16"), "incl": _sb(128, "bfloat16"),
    "excl": _sb(128, "bfloat16"), "prod": _sb(128), "tree": _sb(112), "amat": _sb(1024, "bfloat16"),
    "bhi": _sb(128, "bfloat16"), "blo": _sb(128, "bfloat16"), "req16": _sb(16, "uint16"), "offs": _sb(64, "uint16"),
    "outb": _sb(960), "land": _sb(2048), "rhsf": _sb(64), "foffs": _sb(32, "uint16"), "gat": _sb(512), "ysb": _sb(512),
    "rsf": _sb(512 // NF), "ps": ("psum", [128, 4096], "float32"),
}
SEMAPHORES = ["rqF", "rqN", "rqO", "rsF", "rsC", "rsN", "fq", "fr", "snt", "sid"] + ["s%d" % i for i in range(NPOOL)]
_CACHE = {}


def _plan(T, topo):
    if "p" in _CACHE:
        return _CACHE["p"]
    cores = list(T.cores)
    n = len(cores)
    rk = [topo.rack(topo.host(c)) for c in cores]
    far = [[d for d in range(n) if rk[d] != rk[r] and not topo.may_write(cores[r], cores[d])]
           + [d for d in range(n) if rk[d] != rk[r] and topo.may_write(cores[r], cores[d])] for r in range(n)]
    near = [[d for d in range(n) if rk[d] == rk[r]] for r in range(n)]
    peer = [[d for d in far[r] if topo.may_write(cores[r], cores[d]) and topo.chip(cores[d]) == topo.chip(cores[r])][0]
            for r in range(n)]
    hf, hn, role = [], [], {}
    for r in range(n):
        c0 = cores[r]
        chipc = [c for c in range(NSIM) if topo.host(c) == topo.host(c0) and topo.chip(c) == topo.chip(c0) and c != c0]
        hf.append([c for c in chipc if topo.die(c) != topo.die(c0)][:NF])
        hn.append([c for c in chipc if topo.die(c) == topo.die(c0)][:NF])
        for f in range(NF):
            role[hf[r][f]] = ("F", r, f)
            role[hn[r][f]] = ("N", r, f)
    p = {"cores": cores, "far": far, "near": near, "peer": peer, "hf": hf, "hn": hn, "role": role}
    _CACHE["p"] = p
    return p


def _fused(g, core, topo, items, per, lsem, avoid=0):
    m = 0xFFFF
    for it in items:
        m &= topo.mask(core, it[0])
    e = [1 << b for b in range(16) if (m >> b) & 1 and not (avoid >> b) & 1]
    trs = []
    for i, (d, s, o, rs) in enumerate(items):
        mk = 0
        for b in e[i * per:(i + 1) * per]:
            mk |= b
        rid, pid = topo.addr(d, core)
        trs.append(RemoteDMATransfer(dst_ids=[DstId(rid=rid, pnc=pid)], dma_engine_mask=mk, remote_sem=rs, src=s, dst=o))
    g.remote_dma_fused(trs, local_sem=lsem)
    return per * len(items)


def _oth(P, r):
    return [x for x in P["near"][r] if x != r]


def _kit(T):
    stages = []

    def stage():
        s = [T.sem["s%d" % len(stages)], 0]
        stages.append(s)
        return s

    def done(ins, s, n=1):
        ins.then_inc(s[0], n)
        s[1] += n

    def need(q, *ss):
        for s in ss:
            q.wait_ge(s[0], s[1])

    def one(ins, n=1):
        s = stage()
        done(ins, s, n)
        return s

    return stages, stage, done, need, one


def _lists(g, T, kit, owners, want_f):
    stages, stage, done, need, one = kit
    A = AluOpType
    V, PE = g.vector, g.tensor
    nw = 4 * len(owners)

    def ts(out, in0, s1, op0, s2=None, op1=None):
        if op1 is None:
            return V.tensor_scalar(out, in0, s1, None, op0)
        return V.tensor_scalar(out, in0, s1, s2, op0, op1)

    def tt(out, a, b, op):
        return V.tensor_tensor(out, a, b, op)

    def iw(i):
        return T.iw[:, i * 8:(i + 1) * 8]

    def fw(i):
        return T.fw[:, i * 8:(i + 1) * 8]

    def bank(b, n):
        return T.ps[:, b * 512:b * 512 + n]

    s_d = one(g.iota(T.d128[:], [[1, 128]], 128, -1))
    s_io = one(g.iota(T.io16[:], [[1, 16]], 0, 0, allow_small_or_imprecise_dtypes=True))
    s_kp = one(g.iota(T.kpat[:], [[0, 16], [1, 8]], 0, 0, allow_small_or_imprecise_dtypes=True))
    s_p1 = one(g.iota(T.pat1[:], [[1, 2], [0, 4], [2, 16]], 0, 0, allow_small_or_imprecise_dtypes=True))
    s_pb = stage()
    a = 0
    while a < len(owners):
        b = a + 1
        while b < len(owners) and owners[b] == owners[b - 1] + 1:
            b += 1
        done(g.iota(T.patb[:, a * 4:b * 4], [[1, (b - a) * 4]], owners[a] * 4, 0, allow_small_or_imprecise_dtypes=True), s_pb)
        a = b
    s_v8 = one(g.iota(T.v8[:], [[-16, 8]], 0, 1)) if want_f else None

    need(V, s_d)
    s_c1 = stage()
    done(ts(T.lstr[:], T.d128[:], 128.0, A.is_gt), s_c1)
    done(V.memset(T.ones[:], 1.0), s_c1)
    need(V, s_kp)
    s_rm = one(ts(T.rmask[:], T.kpat[:], 1.0, A.min))

    IOWN, IA, IB, IM, ILO, IO4, IO64, ICNT, IK1, IT, IHB, IJX = range(12)
    FOWN, FT1, FT3, FIB, FLO, FU, FHI, FK1, FK2, FV1, FXB, FVAL = range(12)
    SR, BA = A.arith_shift_right, A.bitwise_and
    V.wait_ge(T.sem.fq, 4)
    s_a = one(ts(iw(IOWN), T.idx_s[:], 13, SR))
    need(V, s_a)
    s_b = one(V.tensor_copy(fw(FOWN), iw(IOWN)))
    need(V, s_b, s_io)
    s_e = stage()
    for k in range(8):
        done(ts(T.e2[:, k:128:8], T.io16[:], T.fw[:, FOWN * 8 + k:FOWN * 8 + k + 1], A.is_equal), s_e)
    need(V, s_e, s_rm)
    s_sc = one(V.tensor_tensor_scan(T.incl[:], T.rmask[:], T.e2[:], 0.0, A.mult, A.add))
    need(V, s_sc)
    s_ex = one(tt(T.excl[:], T.incl[:], T.e2[:], A.subtract))

    need(PE, s_c1, s_e, s_ex)
    s_cm = stage()
    done(PE.matmul(bank(6, 128), T.lstr[:], T.e2[:], True, False), s_cm)
    done(PE.matmul(bank(6, 128), T.ones[:], T.excl[:], False, True), s_cm)

    s_h1 = stage()
    done(ts(iw(IA), T.idx_s[:], 1, BA), s_h1)
    done(ts(iw(IB), T.idx_s[:], 1, SR, 0xE00, BA), s_h1)
    done(ts(iw(IM), T.idx_s[:], 1, SR, 3, BA), s_h1)
    done(ts(iw(ILO), T.idx_s[:], 3, SR, 127, BA), s_h1)
    done(ts(iw(IO4), T.idx_s[:], 11, SR, 60, BA), s_h1)
    done(ts(iw(IO64), T.idx_s[:], 7, SR, 960, BA), s_h1)
    need(V, s_h1)
    s_h2 = stage()
    done(ts(fw(FT1), iw(IA), 4096.0, A.mult), s_h2)
    done(ts(fw(FT3), iw(IM), 128.0, A.mult), s_h2)
    done(V.tensor_copy(fw(FIB), iw(IB)), s_h2)
    done(V.tensor_copy(fw(FLO), iw(ILO)), s_h2)
    need(V, s_h2)
    s_h3 = one(tt(fw(FU), fw(FT1), fw(FT3), A.add))
    need(V, s_h3)
    s_h4 = one(tt(fw(FHI), fw(FU), fw(FIB), A.add))

    need(V, s_cm)
    s_p = one(tt(T.prod[:], bank(6, 128), T.e2[:], A.mult))
    need(V, s_p)
    s_t1 = one(tt(T.tree[:, 0:64], T.prod[:, 0:64], T.prod[:, 64:128], A.add))
    need(V, s_t1)
    s_t2 = one(tt(T.tree[:, 64:96], T.tree[:, 0:32], T.tree[:, 32:64], A.add))
    need(V, s_t2)
    s_t3 = one(tt(T.tree[:, 96:112], T.tree[:, 64:80], T.tree[:, 80:96], A.add))
    need(V, s_t3)
    s_cn = one(tt(iw(ICNT), T.tree[:, 96:104], T.tree[:, 104:112], A.add))
    need(V, s_cn)
    s_k1 = stage()
    done(ts(iw(IK1), iw(ICNT), 31, BA), s_k1)
    done(ts(iw(IT), iw(ICNT), 5, SR), s_k1)
    done(ts(iw(IHB), iw(ICNT), 1, BA), s_k1)
    done(ts(iw(IJX), iw(ICNT), 1, SR), s_k1)
    need(V, s_k1)
    s_k2 = stage()
    done(V.tensor_copy(fw(FK1), iw(IK1)), s_k2)
    done(tt(fw(FK2), iw(IO4), iw(IT), A.add), s_k2)
    need(V, s_k2, s_h4, s_p1, s_pb)
    s_ab = stage()
    for k in range(8):
        def col(i):
            return T.fw[:, i * 8 + k:i * 8 + k + 1]
        done(ts(T.amat[:, k * 128:(k + 1) * 128], T.pat1[:], col(FK1), A.is_equal), s_ab)
        done(ts(T.bhi[:, k * nw:(k + 1) * nw], T.patb[:, 0:nw], col(FK2), A.is_equal, col(FHI), A.mult), s_ab)
        done(ts(T.blo[:, k * nw:(k + 1) * nw], T.patb[:, 0:nw], col(FK2), A.is_equal, col(FLO), A.mult), s_ab)

    need(PE, s_ab)
    s_rm2 = stage()
    for k in range(8):
        done(PE.matmul(bank(7, nw), T.amat[:, k * 128:(k + 1) * 128], T.bhi[:, k * nw:(k + 1) * nw], k == 0, False), s_rm2)
        done(PE.matmul(bank(7, nw), T.amat[:, k * 128:(k + 1) * 128], T.blo[:, k * nw:(k + 1) * nw], False, k == 7), s_rm2)
    need(V, s_rm2)
    s_req = one(V.tensor_copy(T.req16[:, 0:nw], bank(7, nw)))
    if not want_f:
        return s_req, None

    s_k3 = stage()
    done(tt(fw(FV1), iw(IO64), iw(IJX), A.add), s_k3)
    done(ts(T.fw[:, FXB * 8:FXB * 8 + 4], T.iw[:, IHB * 8:IHB * 8 + 4], 1024.0, A.mult), s_k3)
    done(ts(T.fw[:, FXB * 8 + 4:FXB * 8 + 8], T.iw[:, IHB * 8 + 4:IHB * 8 + 8], -1024.0, A.mult, 1024.0, A.add), s_k3)
    need(V, s_v8)
    done(ts(T.v8s[:], T.v8[:], 4, SR), s_k3)
    done(ts(T.amod[:], T.d128[:], 15, BA), s_k3)
    need(V, s_k3)
    s_k4 = stage()
    done(tt(fw(FVAL), fw(FV1), fw(FXB), A.add), s_k4)
    done(ts(T.mask8[:], T.v8s[:], 0.0, A.is_equal), s_k4)
    s_a2 = stage()
    done(ts(T.a2[:, 0:64], T.amod[:, 0:64], 0.0, A.is_equal), s_a2)
    done(ts(T.a2[:, 192:256], T.amod[:, 64:128], 0.0, A.is_equal), s_a2)
    done(V.memset(T.a2[:, 64:192], 0.0), s_a2)
    need(V, s_k4)
    s_rh = stage()
    for k in range(8):
        done(ts(T.rhsf[:, k * 8:(k + 1) * 8], T.mask8[:], T.fw[:, FVAL * 8 + k:FVAL * 8 + k + 1], A.mult), s_rh)
    need(PE, s_rh, s_a2)
    s_fo = stage()
    done(PE.matmul(bank(3, 32), T.a2[:, 0:128], T.rhsf[:, 0:32], True, False), s_fo)
    done(PE.matmul(bank(3, 32), T.a2[:, 128:256], T.rhsf[:, 32:64], False, True), s_fo)
    need(V, s_fo)
    s_ff = one(V.tensor_copy(T.foffs[:], bank(3, 32)))
    return s_req, s_ff


def _helper(g, core, T, topo, P, kind, x, f):
    cores = P["cores"]
    kit = _kit(T)
    stages, need = kit[0], kit[3]
    rq, rs = [], []
    if kind == "F":
        s = P["peer"][x]
        owners = P["far"][s][f * 4:(f + 1) * 4]
        for i, o in enumerate(owners):
            po = P["far"][o].index(s)
            rq.append((cores[o], T.req16[:, i * 4:(i + 1) * 4], T.offs[:, po * 4:po * 4 + 4], T.sem.rqF))
        for i, q in enumerate(P["far"][s][f * 2:(f + 1) * 2]):
            rs.append((cores[q], T.rsf[:, i * 64:(i + 1) * 64], T.land[:, s * 64:(s + 1) * 64], T.sem.rsF))
    else:
        owners = P["near"][x][f * 4:(f + 1) * 4]
        for i, o in enumerate(owners):
            po = 15 if o == x else 8 + _oth(P, o).index(x)
            rq.append((cores[o], T.req16[:, i * 4:(i + 1) * 4], T.offs[:, po * 4:po * 4 + 4], T.sem.rqN))
        for i in range(f, 4):
            q = _oth(P, x)[3 * f + i]
            rs.append((cores[q], T.rsf[:, i * 64:(i + 1) * 64], T.land[:, x * 64:(x + 1) * 64], T.sem.rsN))
    want_f = kind == "N" and f == NF - 1
    s_req, s_ff = _lists(g, T, kit, owners, want_f)
    g.wait_ge(T.sem.fq, 4)
    need(g, s_req)
    sent = _fused(g, core, topo, rq, 2, T.sem.snt)
    if want_f:
        need(g, s_ff)
        sent += _fused(g, core, topo, [(cores[x], T.foffs[:], T.foffs[:], T.sem.rqO)], 4, T.sem.snt)
    g.wait_ge(T.sem.fr, 4)
    sent += _fused(g, core, topo, rs, 4 if kind == "F" else 2, T.sem.snt)
    g.wait_ge(T.sem.snt, sent)
    need(g, *stages)


def rank_program(g, core, T, topo):
    P = _plan(T, topo)
    me = T.rank_of(core)
    if me is None:
        if core in P["role"]:
            _helper(g, core, T, topo, P, *P["role"][core])
        return
    A = AluOpType
    CP = ActivationFunctionType.Copy
    V, S, PE, SY = g.vector, g.scalar, g.tensor, g.sync
    cores, far, near = P["cores"], P["far"][me], P["near"][me]
    stages, stage, done, need, one = _kit(T)

    def bank(b, n):
        return T.ps[:, b * 512:b * 512 + n]

    s_idx = one(SY.dma_start(T.idx_s[:], T.idx[:]), 16)
    s_ld = []
    for b in range(8):
        q = S if b < AHEAD and b % 2 == 1 else SY
        if b == AHEAD:
            SY.wait_ge(T.sem.sid, 16)
        s_ld.append(one(q.dma_start(T.raw[:, b * 512:(b + 1) * 512], T.tab[b * 1024:(b + 1) * 1024, :]), 16))

    s_d = one(g.iota(T.d128[:], [[1, 128]], 128, -1))
    need(V, s_d)
    s_id = one(V.tensor_scalar(T.ident[:], T.d128[:], 128.0, None, A.is_equal))

    sent = 0
    HF = P["hf"][P["peer"][me]]
    HN = P["hn"][me]
    offchip = topo.mask(core, HF[0])
    need(g, s_idx)
    _fused(g, core, topo, [(HF[f], T.idx_s[:], T.idx_s[:], T.sem.fq) for f in range(NF)], 4, T.sem.sid)
    _fused(g, core, topo, [(HN[f], T.idx_s[:], T.idx_s[:], T.sem.fq) for f in range(NF)], 4, T.sem.sid, offchip)

    s_tp = [stage() for _ in GROUPS]
    s_cp = [stage() for _ in GROUPS]
    t0s = [sum(GROUPS[:i]) for i in range(len(GROUPS))]
    ld_seen = [False] * 8

    def transposes(gi, lo, hi):
        for i in range(lo, hi):
            t = t0s[gi] + i
            if not ld_seen[t // 4]:
                need(PE, s_ld[t // 4])
                ld_seen[t // 4] = True
            done(PE.transpose(T.ps[:, GBANK[gi] * 512 + i * 128:GBANK[gi] * 512 + (i + 1) * 128],
                              T.raw[:, t * 128:(t + 1) * 128], T.ident[:]), s_tp[gi])

    def copies(gi):
        n = GROUPS[gi] * 128
        q = S if gi in ON_SCALAR else V
        need(q, s_tp[gi])
        for jj in range(2):
            for h in range(2):
                o = T.win[h * 64:(h + 1) * 64, jj * 4096 + t0s[gi] * 128:jj * 4096 + t0s[gi] * 128 + n]
                i = T.ps[jj * 64:(jj + 1) * 64, GBANK[gi] * 512:GBANK[gi] * 512 + n]
                done(S.activation(o, i, CP) if gi in ON_SCALAR else V.tensor_copy(o, i), s_cp[gi])

    need(PE, s_id)
    for gi in range(len(GROUPS)):
        if gi >= 8:
            need(PE, s_cp[gi - 8])
        transposes(gi, 0, GROUPS[gi])
        copies(gi)

    need(V, *s_cp)
    V.wait_ge(T.sem.rqF, 16)
    s_gd = one(V.tensor_copy(T.outb[:, 0:256], T.win[:, 0:8192].indirect(T.offs[:, 0:16])))
    s_gc = one(V.tensor_copy(T.outb[:, 256:512], T.win[:, 0:8192].indirect(T.offs[:, 16:32])))
    need(S, *s_cp)
    S.wait_ge(T.sem.rqN, 16)
    s_gn = one(S.activation(T.outb[:, 512:960], T.win[:, 0:8192].indirect(T.offs[:, 32:60]), CP))
    V.wait_ge(T.sem.rqN, 16)
    s_go = one(V.tensor_copy(T.land[:, me * 64:(me + 1) * 64], T.win[:, 0:8192].indirect(T.offs[:, 60:64])))
    need(g, s_gd)
    sent += _fused(g, core, topo, [(HF[f], T.outb[:, f * 128:(f + 1) * 128], T.rsf[:, 0:128], T.sem.fr) for f in range(NF)],
                   4, T.sem.snt)
    need(g, s_gn)
    sent += _fused(g, core, topo, [(HN[f], T.outb[:, 512 + f * 192:768 + f * 192], T.rsf[:], T.sem.fr) for f in range(NF)],
                   4, T.sem.snt, offchip)
    need(g, s_gc)
    sent += _fused(g, core, topo, [(cores[q], T.outb[:, (4 + i) * 64:(5 + i) * 64], T.land[:, me * 64:(me + 1) * 64],
                                    T.sem.rsC) for i, q in enumerate(far[4:8])], 2, T.sem.snt)

    def runs(lst):
        out = []
        for x in sorted(lst):
            if out and out[-1][1] == x:
                out[-1][1] = x + 1
            else:
                out.append([x, x + 1])
        return out

    s_du = stage()
    need(V, s_go)
    need(S, s_go)
    for sem, cnt, lst in ((T.sem.rsN, 14, near), (T.sem.rsC, 8, far[4:8]), (T.sem.rsF, 16, far[0:4])):
        V.wait_ge(sem, cnt)
        S.wait_ge(sem, cnt)
        for lo, hi in runs(lst):
            done(V.tensor_copy(T.land[0:64, 1024 + lo * 64:1024 + hi * 64], T.land[64:128, lo * 64:hi * 64]), s_du)
            done(S.activation(T.land[64:128, 1024 + lo * 64:1024 + hi * 64], T.land[0:64, lo * 64:hi * 64], CP), s_du)
    need(V, s_du)
    V.wait_ge(T.sem.rqO, 4)
    s_g = [one(V.tensor_copy(T.gat[:, kk * 128:(kk + 1) * 128],
                             T.land[:, 0:2048].indirect(T.foffs[:, kk * 8:(kk + 1) * 8]))) for kk in range(4)]
    s_st = stage()
    for kk in range(4):
        need(PE, s_g[kk])
        s_t = one(PE.transpose(bank(4 + kk, 128), T.gat[:, kk * 128:(kk + 1) * 128], T.ident[:]))
        o = T.ysb[:, kk * 128:(kk + 1) * 128]
        if kk % 2 == 0:
            need(V, s_t)
            s_y = one(V.tensor_copy(o, bank(4 + kk, 128)))
            q = SY
        else:
            need(S, s_t)
            s_y = one(S.activation(o, bank(4 + kk, 128), CP))
            q = S
        need(q, s_y)
        for hh in range(2):
            r0 = (hh * 4 + kk) * 128
            done(q.dma_start(T.y[r0:r0 + 128, :], T.ysb[:, kk * 128 + hh * 64:kk * 128 + hh * 64 + 64]), s_st, 16)

    g.wait_ge(T.sem.sid, 16)
    g.wait_ge(T.sem.snt, sent)
    need(g, *stages)
